import numpy as np
import ml_dtypes


def mxq(x, axis, fmt="e4m3"):
    dtype, down = {"e4m3": (ml_dtypes.float8_e4m3fn, 7), "e5m2": (ml_dtypes.float8_e5m2, 14)}[fmt]
    v = np.moveaxis(np.asarray(x, np.float32).astype(ml_dtypes.bfloat16).astype(np.float64), axis, -1)
    blocks = v.reshape(v.shape[:-1] + (-1, 32))
    amax = np.abs(blocks).max(-1, keepdims=True)
    byte = np.maximum(np.where(amax > 0, np.frexp(amax)[1] - 1 + 127, 0) - down, 1)
    scale = np.exp2(byte - 127.0)
    codes = (blocks / scale).astype(np.float32).astype(dtype).astype(np.float64)
    return np.moveaxis((codes * scale).reshape(v.shape), -1, axis)


WIDE = False


def mx_kscale(k):
    if not WIDE:
        return np.ones(k)
    levels = np.array([10, -10, 5, -5, 0])
    if k % 512:
        return np.exp2(np.random.permutation(np.resize(levels, k // 32))).repeat(32)
    a = np.empty((k // 512, 16))
    for p in range(k // 512):
        a[p, :8] = np.random.permutation(np.resize(levels, 8))
        for g in range(8):
            far = levels[np.abs(levels - a[p, g]) >= 10]
            a[p, g + 8] = far[np.random.randint(len(far))]
    return np.exp2(a.ravel()).repeat(32)


def f64(x):
    return np.asarray(x).astype(np.float64)


E2M1 = np.array([0.0, 0.5, 1.0, 1.5, 2.0, 3.0, 4.0, 6.0, -0.0, -0.5, -1.0, -1.5, -2.0, -3.0, -4.0, -6.0])


def pack_weight(w, fmt):
    k, n = w.shape
    w = f64(np.asarray(w, np.float32).astype(ml_dtypes.bfloat16)).reshape(k // 32, 32, n)
    amax = np.abs(w).max(1)
    if fmt == "e4m3":
        byte = np.frexp(amax)[1] - 1 + 127 - 7
    else:
        mant, ex = np.frexp(amax / 6.0)
        byte = np.where(mant > 0.5, ex, ex - 1) + 127
    byte = np.clip(np.where(amax > 0, byte, 1), 1, 254)
    scaled = (w * np.exp2(127.0 - byte)[:, None, :]).reshape(k, n).astype(np.float32)
    by_word = np.ascontiguousarray(scaled.reshape(k // 512, 128, 4, n).transpose(0, 1, 3, 2))
    if fmt == "e4m3":
        words = by_word.astype(ml_dtypes.float8_e4m3fn).view(np.uint8)
    else:
        c = by_word.astype(ml_dtypes.float4_e2m1fn).view(np.uint8) & 0xF
        words = (c[..., 0::2] | (c[..., 1::2] << 4)).reshape(k // 512, 128, 2 * n)
    return np.ascontiguousarray(words), np.ascontiguousarray(byte.astype(np.uint8).reshape(k // 512, 16, n))


def unpack_weight(words, scales, fmt):
    g, _, n = scales.shape
    words = np.ascontiguousarray(words).reshape(g, 128, n, -1)
    if fmt == "e4m3":
        vals = words.view(ml_dtypes.float8_e4m3fn).astype(np.float64)
    else:
        nib = np.empty((g, 128, n, 4), np.uint8)
        nib[..., 0::2] = words & 0xF
        nib[..., 1::2] = words >> 4
        vals = E2M1[nib]
    vals = vals * np.repeat(np.exp2(scales.astype(np.float64) - 127.0), 8, axis=1)[..., None]
    return vals.transpose(0, 1, 3, 2).reshape(g * 512, n)


K, R, M, T = 1024, 512, 1024, 1024


def setup_inputs():
    n = np.random.standard_normal
    s = mx_kscale(K)[:, None]
    u = mx_kscale(R)[:, None]
    p_w4 = pack_weight(n((K, M)) / np.sqrt(K) / s, "e2m1")
    return {
        "x": (n((K, T)) * s).astype(np.float32),
        "w4_words": p_w4[0],
        "w4_scales": p_w4[1],
        "down": (n((K, R)) / np.sqrt(K) / s * u.T).astype(np.float32),
        "up": (0.5 * n((R, M)) / np.sqrt(R) / u).astype(np.float32),
    }


def reference(x, w4_words, w4_scales, down, up):
    x_ = mxq(f64(x), 0, "e4m3")
    w4_ = unpack_weight(w4_words, w4_scales, "e2m1")
    down_ = mxq(f64(down), 0, "e4m3")
    up_ = mxq(f64(up), 0, "e4m3")
    h_ = mxq(down_.T @ x_, 0, "e4m3")
    y = x_.T @ w4_ + h_.T @ up_
    return y

@@ -1,0 +1,295 @@
+from contextlib import ExitStack
+
+import concourse.mybir as mybir
+
+K, R, N, T = 1024, 512, 1024, 1024
+FLOPS = 2 * (K * R * T + K * N * T + R * N * T)
+
+F32 = mybir.dt.float32
+BF16 = mybir.dt.bfloat16
+I32 = mybir.dt.int32
+U32 = mybir.dt.uint32
+U8 = mybir.dt.uint8
+E4M3 = mybir.dt.float8_e4m3fn_x4
+E2M1 = mybir.dt.float4_e2m1fn_x4
+
+P = 128
+PACK = 4
+K_PASSES = K // (P * PACK)
+X_COLS = 256
+UP_COLS = 256
+HALF = 512
+T_TILES = T // P
+DOWN_SPLIT = 88
+X_SPLIT = {(0, 0): 256, (0, 1): 176, (1, 0): 128, (1, 1): 176, (2, 0): 256, (2, 1): 256, (3, 0): 256, (3, 1): 256}
+UP_SPLIT = {0: 256, 1: 176, 2: 256, 3: 256}
+
+
+def tile_mix_lowrank_tm_none_kernel(tc, x, w4_words, w4_scales, down, up, out):
+    nc = tc.nc
+    with ExitStack() as ctx:
+        keep = ctx.enter_context(tc.tile_pool(name="keep", bufs=1))
+        acc_pool = ctx.enter_context(tc.psum_pool(name="acc", bufs=1))
+        h_pool = ctx.enter_context(tc.psum_pool(name="hps", bufs=2))
+        ctx.enter_context(tc.manual_schedule())
+
+        def sb(name, shape, dtype):
+            return keep.tile(shape, dtype, name=name, tag=name, align_bytes=64)
+
+        w4c = sb("w4c", [P, K_PASSES, 2 * N], U8)
+        w4s = sb("w4s", [P, K_PASSES, N], U8)
+        nc.vector.memset(w4s[:].rearrange("p g n -> p (g n)").bitcast(I32), 0)
+
+        x_raw, x_grp, x_codes, x_scales = {}, {}, {}, {}
+
+        def load_x(c, g):
+            raw = sb(f"xr{c}_{g}", [P, PACK, X_COLS], F32)
+            rows = x[g * 512 : (g + 1) * 512, c * X_COLS : (c + 1) * X_COLS]
+            nc.sync.dma_start(out=raw[:], in_=rows.rearrange("(p j) w -> p j w", j=PACK))
+            x_raw[c, g] = raw
+
+        d_raw, d_grp, d_codes, d_scales = {}, {}, {}, {}
+
+        def load_down(g):
+            raw = sb(f"dr{g}", [P, PACK, R], F32)
+            nc.sync.dma_start(out=raw[:], in_=down[g * 512 : (g + 1) * 512, :].rearrange("(p j) r -> p j r", j=PACK))
+            d_raw[g] = raw
+
+        u_raw, u_grp = {}, {}
+        u_codes = [sb(f"uc{i}", [P, HALF], U32) for i in range(2)]
+        u_scales = [sb(f"us{i}", [P, HALF], U8) for i in range(2)]
+
+        def load_up(q):
+            raw = sb(f"ur{q}", [P, PACK, UP_COLS], F32)
+            rows = up[:, q * UP_COLS : (q + 1) * UP_COLS]
+            nc.sync.dma_start(out=raw[:], in_=rows.rearrange("(p j) w -> p j w", j=PACK))
+            u_raw[q] = raw
+
+        load_x(0, 0)
+        for g in range(K_PASSES):
+            nc.sync.dma_start(out=w4c[:, g, :].bitcast(I32), in_=w4_words[g].bitcast(I32))
+        load_x(0, 1)
+        for q in range(4):
+            nc.scalar.dma_start(
+                out=w4s[32 * q : 32 * q + 4].bitcast(I32),
+                in_=w4_scales[:, 4 * q : 4 * q + 4, :].rearrange("g q n -> q g n").bitcast(I32),
+            )
+        load_down(0)
+        load_down(1)
+        load_x(1, 0)
+        load_x(1, 1)
+        load_up(0)
+        load_up(1)
+        for c in (2, 3):
+            load_x(c, 0)
+            load_x(c, 1)
+        load_up(2)
+        load_up(3)
+
+        def interleave(grp, raw, split):
+            src = raw[:].rearrange("p j w -> p w j")
+            nc.vector.tensor_copy(out=grp[:, :split], in_=src[:, :split])
+            if split < src.shape[1]:
+                nc.scalar.copy(out=grp[:, split:], in_=src[:, split:])
+
+        def copy_x(c, g):
+            grp = sb(f"xg{c}_{g}", [P, X_COLS, PACK], BF16)
+            interleave(grp, x_raw[c, g], X_SPLIT[c, g])
+            x_grp[c, g] = grp
+
+        def quant_x(c, g):
+            codes = sb(f"xc{c}_{g}", [P, X_COLS], U32)
+            scales = sb(f"xs{c}_{g}", [P, X_COLS], U8)
+            nc.vector.quantize_mx(
+                out=codes[:].bitcast(E4M3), scales=scales[:], in_=x_grp[c, g][:].rearrange("p w j -> p (w j)")
+            )
+            x_codes[c, g], x_scales[c, g] = codes, scales
+
+        def copy_down(g):
+            grp = sb(f"dg{g}", [P, PACK, P, PACK], BF16)
+            src = d_raw[g][:].rearrange("p j (m i) -> p m i j", i=PACK)
+            dst = grp[:].rearrange("p i m j -> p m i j")
+            nc.vector.tensor_copy(out=dst[:, :DOWN_SPLIT], in_=src[:, :DOWN_SPLIT])
+            nc.scalar.copy(out=dst[:, DOWN_SPLIT:], in_=src[:, DOWN_SPLIT:])
+            d_grp[g] = grp
+
+        def quant_down(g):
+            codes = sb(f"dc{g}", [P, R], U32)
+            scales = sb(f"ds{g}", [P, R], U8)
+            nc.vector.quantize_mx(
+                out=codes[:].bitcast(E4M3), scales=scales[:], in_=d_grp[g][:].rearrange("p i m j -> p (i m j)")
+            )
+            d_codes[g], d_scales[g] = codes, scales
+
+        def copy_up(q):
+            grp = sb(f"ug{q}", [P, UP_COLS, PACK], BF16)
+            interleave(grp, u_raw[q], UP_SPLIT[q])
+            u_grp[q] = grp
+
+        def quant_up(q):
+            cols = slice((q % 2) * UP_COLS, (q % 2 + 1) * UP_COLS)
+            nc.vector.quantize_mx(
+                out=u_codes[q // 2][:, cols].bitcast(E4M3),
+                scales=u_scales[q // 2][:, cols],
+                in_=u_grp[q][:].rearrange("p w j -> p (w j)"),
+            )
+
+        acc = {}
+        bank_of = {
+            (0, 0): 0, (1, 0): 1, (2, 0): 2, (3, 0): 0, (4, 0): 1, (5, 0): 2, (6, 0): 0, (7, 0): 1,
+            (0, 1): 3, (1, 1): 4, (2, 1): 5, (3, 1): 2, (4, 1): 0, (5, 1): 1, (6, 1): 3, (7, 1): 4,
+        }
+
+        def x_view(t, g):
+            c, first = divmod(t * P, X_COLS)
+            cols = slice(first, first + P)
+            return x_codes[c, g][:, cols].bitcast(E4M3), x_scales[c, g][:, cols]
+
+        def base(t, n, g):
+            if g == 0:
+                b = bank_of[t, n]
+                acc[t, n] = acc_pool.tile([P, HALF], F32, name=f"acc{t}_{n}", tag=f"b{b}")
+            codes, scales = x_view(t, g)
+            nc.tensor.matmul_mx(
+                out=acc[t, n][:],
+                lhsT=codes,
+                lhsT_scale=scales,
+                rhs=w4c[:, g, 2 * HALF * n : 2 * HALF * (n + 1)].bitcast(E2M1),
+                rhs_scale=w4s[:, g, HALF * n : HALF * (n + 1)],
+                start=(g == 0),
+                stop=False,
+            )
+
+        h_codes, h_scales, h_ps, h_grp = {}, {}, {}, {}
+
+        def branch(t, n):
+            nc.tensor.matmul_mx(
+                out=acc[t, n][:],
+                lhsT=h_codes[t][:].bitcast(E4M3),
+                lhsT_scale=h_scales[t][:],
+                rhs=u_codes[n][:].bitcast(E4M3),
+                rhs_scale=u_scales[n][:],
+                start=False,
+                stop=True,
+            )
+
+        def make_h(t):
+            ps = h_pool.tile([P, PACK, P], F32, name=f"hp{t}", tag="hp")
+            for i in range(PACK):
+                cols = slice(i * P, (i + 1) * P)
+                for g in range(K_PASSES):
+                    codes, scales = x_view(t, g)
+                    nc.tensor.matmul_mx(
+                        out=ps[:, i, :],
+                        lhsT=d_codes[g][:, cols].bitcast(E4M3),
+                        lhsT_scale=d_scales[g][:, cols],
+                        rhs=codes,
+                        rhs_scale=scales,
+                        start=(g == 0),
+                        stop=(g == K_PASSES - 1),
+                    )
+            h_ps[t] = ps
+
+        def copy_h(t):
+            grp = sb(f"hg{t}", [P, P, PACK], BF16)
+            nc.scalar.copy(out=grp[:], in_=h_ps[t][:].rearrange("p i t -> p t i"))
+            h_grp[t] = grp
+
+        def quant_h(t):
+            codes = sb(f"hc{t}", [P, P], U32)
+            scales = sb(f"hs{t}", [P, P], U8)
+            nc.vector.quantize_mx(
+                out=codes[:].bitcast(E4M3), scales=scales[:], in_=h_grp[t][:].rearrange("p t i -> p (t i)")
+            )
+            h_codes[t], h_scales[t] = codes, scales
+
+        def finish(t, n, engine):
+            res = sb(f"o{t}_{n}", [P, HALF], F32)
+            if engine == "scalar":
+                nc.scalar.copy(out=res[:], in_=acc[t, n][:])
+            else:
+                nc.vector.tensor_copy(out=res[:], in_=acc[t, n][:])
+            nc.sync.dma_start(out=out[t * P : (t + 1) * P, n * HALF : (n + 1) * HALF], in_=res[:])
+
+        for g in range(K_PASSES):
+            copy_x(0, g)
+            quant_x(0, g)
+        for g in range(K_PASSES):
+            for t in (0, 1):
+                base(t, 0, g)
+                base(t, 1, g)
+        for g in range(K_PASSES):
+            copy_down(g)
+            quant_down(g)
+        copy_x(1, 0)
+        copy_x(1, 1)
+        quant_x(1, 0)
+        quant_x(1, 1)
+        make_h(0)
+        copy_h(0)
+        make_h(1)
+        copy_h(1)
+        for g in range(K_PASSES):
+            base(2, 0, g)
+            base(2, 1, g)
+        quant_h(0)
+        quant_h(1)
+        copy_up(0)
+        copy_up(1)
+        quant_up(0)
+        quant_up(1)
+        make_h(2)
+        copy_h(2)
+        make_h(3)
+        copy_h(3)
+        quant_h(2)
+        copy_x(2, 0)
+        quant_h(3)
+        copy_x(2, 1)
+        quant_x(2, 0)
+        quant_x(2, 1)
+        for t in (0, 1, 2):
+            branch(t, 0)
+            finish(t, 0, "scalar")
+        base(3, 0, 0)
+        base(3, 0, 1)
+        branch(3, 0)
+        copy_x(3, 0)
+        make_h(4)
+        copy_h(4)
+        make_h(5)
+        copy_h(5)
+        finish(3, 0, "scalar")
+        copy_x(3, 1)
+        quant_x(3, 0)
+        quant_h(4)
+        quant_x(3, 1)
+        quant_h(5)
+        for t in (4, 5):
+            base(t, 0, 0)
+            base(t, 0, 1)
+        for t in (4, 5):
+            branch(t, 0)
+            finish(t, 0, "scalar")
+        make_h(6)
+        copy_h(6)
+        make_h(7)
+        copy_h(7)
+        copy_up(2)
+        copy_up(3)
+        quant_up(2)
+        quant_h(6)
+        quant_up(3)
+        quant_h(7)
+        for t in (6, 7):
+            base(t, 0, 0)
+            base(t, 0, 1)
+        for t in (6, 7):
+            branch(t, 0)
+            finish(t, 0, "scalar" if t % 2 == 0 else "vector")
+        for t in range(T_TILES):
+            if t >= 3:
+                base(t, 1, 0)
+                base(t, 1, 1)
+            branch(t, 1)
+            finish(t, 1, "scalar" if t % 2 == 0 else "vector")

@@ -20,17 +20,15 @@ X_COLS = 256
 UP_COLS = 256
 HALF = 512
 T_TILES = T // P
-DOWN_SPLIT = 88
-X_SPLIT = {(0, 0): 256, (0, 1): 176, (1, 0): 128, (1, 1): 176, (2, 0): 256, (2, 1): 256, (3, 0): 256, (3, 1): 256}
-UP_SPLIT = {0: 256, 1: 176, 2: 256, 3: 256}
+DOWN_SPLIT = 64
 
 
 def tile_mix_lowrank_tm_none_kernel(tc, x, w4_words, w4_scales, down, up, out):
     nc = tc.nc
+    S, V = "scalar", "vector"
     with ExitStack() as ctx:
         keep = ctx.enter_context(tc.tile_pool(name="keep", bufs=1))
         acc_pool = ctx.enter_context(tc.psum_pool(name="acc", bufs=1))
-        h_pool = ctx.enter_context(tc.psum_pool(name="hps", bufs=2))
         ctx.enter_context(tc.manual_schedule())
 
         def sb(name, shape, dtype):
@@ -65,36 +63,43 @@ def tile_mix_lowrank_tm_none_kernel(tc, x, w4_words, w4_scales, down, up, out):
             nc.sync.dma_start(out=raw[:], in_=rows.rearrange("(p j) w -> p j w", j=PACK))
             u_raw[q] = raw
 
+        load_down(0)
         load_x(0, 0)
-        for g in range(K_PASSES):
-            nc.sync.dma_start(out=w4c[:, g, :].bitcast(I32), in_=w4_words[g].bitcast(I32))
         load_x(0, 1)
+        load_down(1)
         for q in range(4):
-            nc.scalar.dma_start(
+            nc.sync.dma_start(
                 out=w4s[32 * q : 32 * q + 4].bitcast(I32),
                 in_=w4_scales[:, 4 * q : 4 * q + 4, :].rearrange("g q n -> q g n").bitcast(I32),
             )
-        load_down(0)
-        load_down(1)
+        nc.sync.dma_start(out=w4c[:].bitcast(I32), in_=w4_words.rearrange("g p n -> p g n").bitcast(I32))
         load_x(1, 0)
         load_x(1, 1)
         load_up(0)
         load_up(1)
-        for c in (2, 3):
-            load_x(c, 0)
-            load_x(c, 1)
+        load_x(2, 0)
+        load_x(2, 1)
+        load_x(3, 0)
         load_up(2)
         load_up(3)
+        load_x(3, 1)
 
-        def interleave(grp, raw, split):
-            src = raw[:].rearrange("p j w -> p w j")
-            nc.vector.tensor_copy(out=grp[:, :split], in_=src[:, :split])
-            if split < src.shape[1]:
-                nc.scalar.copy(out=grp[:, split:], in_=src[:, split:])
+        def copy(engine, out, in_):
+            if engine == S:
+                nc.scalar.copy(out=out, in_=in_)
+            else:
+                nc.vector.tensor_copy(out=out, in_=in_)
 
-        def copy_x(c, g):
+        def interleave(engine, grp, raw):
+            copy(
+                engine,
+                grp[:].rearrange("p (c i) j -> p c j i", i=4),
+                raw[:].rearrange("p j (c i) -> p c j i", i=4),
+            )
+
+        def copy_x(c, g, engine):
             grp = sb(f"xg{c}_{g}", [P, X_COLS, PACK], BF16)
-            interleave(grp, x_raw[c, g], X_SPLIT[c, g])
+            interleave(engine, grp, x_raw[c, g])
             x_grp[c, g] = grp
 
         def quant_x(c, g):
@@ -121,9 +126,9 @@ def tile_mix_lowrank_tm_none_kernel(tc, x, w4_words, w4_scales, down, up, out):
             )
             d_codes[g], d_scales[g] = codes, scales
 
-        def copy_up(q):
+        def copy_up(q, engine):
             grp = sb(f"ug{q}", [P, UP_COLS, PACK], BF16)
-            interleave(grp, u_raw[q], UP_SPLIT[q])
+            interleave(engine, grp, u_raw[q])
             u_grp[q] = grp
 
         def quant_up(q):
@@ -136,29 +141,29 @@ def tile_mix_lowrank_tm_none_kernel(tc, x, w4_words, w4_scales, down, up, out):
 
         acc = {}
         bank_of = {
-            (0, 0): 0, (1, 0): 1, (2, 0): 2, (3, 0): 0, (4, 0): 1, (5, 0): 2, (6, 0): 0, (7, 0): 1,
-            (0, 1): 3, (1, 1): 4, (2, 1): 5, (3, 1): 2, (4, 1): 0, (5, 1): 1, (6, 1): 3, (7, 1): 4,
+            (0, 0): 0, (1, 0): 4, (2, 0): 6, (3, 0): 2, (4, 0): 0, (5, 0): 4, (6, 0): 2, (7, 0): 1,
+            (0, 1): 1, (1, 1): 5, (2, 1): 3, (3, 1): 7, (4, 1): 6, (5, 1): 3, (6, 1): 7, (7, 1): 6,
         }
+        h_bank = [2, 3, 3, 2, 0, 2, 2, 5]
 
         def x_view(t, g):
             c, first = divmod(t * P, X_COLS)
             cols = slice(first, first + P)
             return x_codes[c, g][:, cols].bitcast(E4M3), x_scales[c, g][:, cols]
 
-        def base(t, n, g):
-            if g == 0:
-                b = bank_of[t, n]
-                acc[t, n] = acc_pool.tile([P, HALF], F32, name=f"acc{t}_{n}", tag=f"b{b}")
-            codes, scales = x_view(t, g)
-            nc.tensor.matmul_mx(
-                out=acc[t, n][:],
-                lhsT=codes,
-                lhsT_scale=scales,
-                rhs=w4c[:, g, 2 * HALF * n : 2 * HALF * (n + 1)].bitcast(E2M1),
-                rhs_scale=w4s[:, g, HALF * n : HALF * (n + 1)],
-                start=(g == 0),
-                stop=False,
-            )
+        def base(t, n):
+            acc[t, n] = acc_pool.tile([P, HALF], F32, name=f"acc{t}_{n}", tag=f"b{bank_of[t, n]}")
+            for g in range(K_PASSES):
+                codes, scales = x_view(t, g)
+                nc.tensor.matmul_mx(
+                    out=acc[t, n][:],
+                    lhsT=codes,
+                    lhsT_scale=scales,
+                    rhs=w4c[:, g, 2 * HALF * n : 2 * HALF * (n + 1)].bitcast(E2M1),
+                    rhs_scale=w4s[:, g, HALF * n : HALF * (n + 1)],
+                    start=(g == 0),
+                    stop=False,
+                )
 
         h_codes, h_scales, h_ps, h_grp = {}, {}, {}, {}
 
@@ -174,7 +179,7 @@ def tile_mix_lowrank_tm_none_kernel(tc, x, w4_words, w4_scales, down, up, out):
             )
 
         def make_h(t):
-            ps = h_pool.tile([P, PACK, P], F32, name=f"hp{t}", tag="hp")
+            ps = acc_pool.tile([P, PACK, P], F32, name=f"hp{t}", tag=f"b{h_bank[t]}")
             for i in range(PACK):
                 cols = slice(i * P, (i + 1) * P)
                 for g in range(K_PASSES):
@@ -190,9 +195,9 @@ def tile_mix_lowrank_tm_none_kernel(tc, x, w4_words, w4_scales, down, up, out):
                     )
             h_ps[t] = ps
 
-        def copy_h(t):
+        def copy_h(t, engine):
             grp = sb(f"hg{t}", [P, P, PACK], BF16)
-            nc.scalar.copy(out=grp[:], in_=h_ps[t][:].rearrange("p i t -> p t i"))
+            copy(engine, grp[:], h_ps[t][:].rearrange("p i t -> p t i"))
             h_grp[t] = grp
 
         def quant_h(t):
@@ -203,93 +208,111 @@ def tile_mix_lowrank_tm_none_kernel(tc, x, w4_words, w4_scales, down, up, out):
             )
             h_codes[t], h_scales[t] = codes, scales
 
-        def finish(t, n, engine):
-            res = sb(f"o{t}_{n}", [P, HALF], F32)
-            if engine == "scalar":
-                nc.scalar.copy(out=res[:], in_=acc[t, n][:])
-            else:
-                nc.vector.tensor_copy(out=res[:], in_=acc[t, n][:])
-            nc.sync.dma_start(out=out[t * P : (t + 1) * P, n * HALF : (n + 1) * HALF], in_=res[:])
+        def finish(t, n, engine, parts=1):
+            width = HALF // parts
+            for i in range(parts):
+                res = sb(f"o{t}_{n}_{i}", [P, width], F32)
+                copy(engine, res[:], acc[t, n][:, i * width : (i + 1) * width])
+                first = n * HALF + i * width
+                nc.sync.dma_start(out=out[t * P : (t + 1) * P, first : first + width], in_=res[:])
 
-        for g in range(K_PASSES):
-            copy_x(0, g)
-            quant_x(0, g)
-        for g in range(K_PASSES):
-            for t in (0, 1):
-                base(t, 0, g)
-                base(t, 1, g)
-        for g in range(K_PASSES):
-            copy_down(g)
-            quant_down(g)
-        copy_x(1, 0)
-        copy_x(1, 1)
-        quant_x(1, 0)
-        quant_x(1, 1)
+        copy_down(0)
+        quant_down(0)
+        copy_x(0, 0, S)
+        copy_x(0, 1, V)
+        quant_x(0, 0)
+        quant_x(0, 1)
+        copy_down(1)
+        base(0, 0)
+        quant_down(1)
+        base(0, 1)
+        copy_x(1, 0, S)
         make_h(0)
-        copy_h(0)
+        copy_x(1, 1, V)
         make_h(1)
-        copy_h(1)
-        for g in range(K_PASSES):
-            base(2, 0, g)
-            base(2, 1, g)
+        copy_h(0, S)
+        base(1, 0)
+        quant_x(1, 0)
+        copy_h(1, S)
+        base(1, 1)
+        quant_x(1, 1)
         quant_h(0)
+        copy_up(0, S)
         quant_h(1)
-        copy_up(0)
-        copy_up(1)
+        base(2, 0)
+        copy_up(1, V)
+        base(3, 1)
+        make_h(3)
         quant_up(0)
+        copy_x(2, 0, S)
         quant_up(1)
         make_h(2)
-        copy_h(2)
-        make_h(3)
-        copy_h(3)
-        quant_h(2)
-        copy_x(2, 0)
+        copy_h(3, V)
+        branch(0, 0)
+        branch(1, 0)
+        copy_x(2, 1, V)
+        copy_h(2, S)
+        base(3, 0)
         quant_h(3)
-        copy_x(2, 1)
-        quant_x(2, 0)
-        quant_x(2, 1)
-        for t in (0, 1, 2):
-            branch(t, 0)
-            finish(t, 0, "scalar")
-        base(3, 0, 0)
-        base(3, 0, 1)
+        finish(0, 0, S)
+        quant_h(2)
         branch(3, 0)
-        copy_x(3, 0)
+        quant_x(2, 0)
+        branch(2, 0)
+        finish(1, 0, S)
+        quant_x(2, 1)
+        base(2, 1)
+        copy_up(2, V)
+        finish(2, 0, S)
         make_h(4)
-        copy_h(4)
-        make_h(5)
-        copy_h(5)
-        finish(3, 0, "scalar")
-        copy_x(3, 1)
-        quant_x(3, 0)
-        quant_h(4)
-        quant_x(3, 1)
-        quant_h(5)
-        for t in (4, 5):
-            base(t, 0, 0)
-            base(t, 0, 1)
-        for t in (4, 5):
-            branch(t, 0)
-            finish(t, 0, "scalar")
-        make_h(6)
-        copy_h(6)
-        make_h(7)
-        copy_h(7)
-        copy_up(2)
-        copy_up(3)
+        finish(3, 0, S)
+        base(5, 0)
         quant_up(2)
-        quant_h(6)
+        base(4, 1)
+        copy_up(3, V)
+        copy_h(4, S)
+        make_h(5)
+        copy_x(3, 0, S)
         quant_up(3)
+        base(4, 0)
+        quant_h(4)
+        copy_x(3, 1, V)
+        branch(3, 1)
+        branch(2, 1)
+        copy_h(5, S)
+        quant_x(3, 0)
+        branch(0, 1)
+        branch(1, 1)
+        quant_x(3, 1)
+        finish(3, 1, S)
+        branch(4, 1)
+        finish(1, 1, V)
+        branch(4, 0)
+        finish(0, 1, S)
+        make_h(6)
+        quant_h(5)
+        base(6, 1)
+        finish(4, 1, S)
+        copy_h(6, V)
+        make_h(7)
+        finish(2, 1, S)
+        quant_h(6)
+        base(7, 0)
+        copy_h(7, S)
+        branch(6, 1)
+        base(7, 1)
+        finish(4, 0, S)
+        finish(6, 1, V)
+        branch(5, 0)
         quant_h(7)
-        for t in (6, 7):
-            base(t, 0, 0)
-            base(t, 0, 1)
-        for t in (6, 7):
-            branch(t, 0)
-            finish(t, 0, "scalar" if t % 2 == 0 else "vector")
-        for t in range(T_TILES):
-            if t >= 3:
-                base(t, 1, 0)
-                base(t, 1, 1)
-            branch(t, 1)
-            finish(t, 1, "scalar" if t % 2 == 0 else "vector")
+        base(5, 1)
+        finish(5, 0, S)
+        branch(7, 1)
+        branch(7, 0)
+        finish(7, 1, V)
+        branch(5, 1)
+        finish(7, 0, S)
+        base(6, 0)
+        finish(5, 1, V)
+        branch(6, 0)
+        finish(6, 0, V, parts=2)

@@ -15,64 +15,195 @@ E2M1 = mybir.dt.float4_e2m1fn_x4
 
 P = 128
 PACK = 4
-K_PASSES = K // (P * PACK)
-X_COLS = 256
-UP_COLS = 256
+ROWS = P * PACK
+K_PASSES = K // ROWS
+WIDTH = 256
+TILES_IN_CHUNK = WIDTH // P
 HALF = 512
-T_TILES = T // P
-DOWN_SPLIT = 64
+BANKS = 8
 
 
 def tile_mix_lowrank_tm_none_kernel(tc, x, w4_words, w4_scales, down, up, out):
     nc = tc.nc
-    S, V = "scalar", "vector"
+    SCALAR, VECTOR = "scalar", "vector"
+
     with ExitStack() as ctx:
         keep = ctx.enter_context(tc.tile_pool(name="keep", bufs=1))
-        acc_pool = ctx.enter_context(tc.psum_pool(name="acc", bufs=1))
+        psum = ctx.enter_context(tc.psum_pool(name="psum", bufs=1))
         ctx.enter_context(tc.manual_schedule())
 
-        def sb(name, shape, dtype):
+        def sbuf(name, shape, dtype):
             return keep.tile(shape, dtype, name=name, tag=name, align_bytes=64)
 
-        w4c = sb("w4c", [P, K_PASSES, 2 * N], U8)
-        w4s = sb("w4s", [P, K_PASSES, N], U8)
-        nc.vector.memset(w4s[:].rearrange("p g n -> p (g n)").bitcast(I32), 0)
+        free_banks = list(range(BANKS))
+        bank_of = {}
 
-        x_raw, x_grp, x_codes, x_scales = {}, {}, {}, {}
+        def take_bank(key, name, shape):
+            bank_of[key] = free_banks[0]
+            free_banks.remove(bank_of[key])
+            return psum.tile(shape, F32, name=name, tag=f"bank{bank_of[key]}")
+
+        def give_back(key):
+            free_banks.append(bank_of[key])
+
+        def copy(engine, dst, src):
+            if engine == SCALAR:
+                nc.scalar.copy(out=dst, in_=src)
+            else:
+                nc.vector.tensor_copy(out=dst, in_=src)
+
+        def quantise(name, width, grouped):
+            codes = sbuf(f"{name}_codes", [P, width], U32)
+            scales = sbuf(f"{name}_scales", [P, width], U8)
+            nc.vector.quantize_mx(out=codes[:].bitcast(E4M3), scales=scales[:], in_=grouped)
+            return codes, scales
+
+        def interleave(engine, grouped, raw):
+            copy(
+                engine,
+                grouped.rearrange("p (c i) j -> p c j i", i=4),
+                raw.rearrange("p j (c i) -> p c j i", i=4),
+            )
+
+        x_raw, x_grouped, x_mx = {}, {}, {}
 
         def load_x(c, g):
-            raw = sb(f"xr{c}_{g}", [P, PACK, X_COLS], F32)
-            rows = x[g * 512 : (g + 1) * 512, c * X_COLS : (c + 1) * X_COLS]
-            nc.sync.dma_start(out=raw[:], in_=rows.rearrange("(p j) w -> p j w", j=PACK))
-            x_raw[c, g] = raw
+            x_raw[c, g] = sbuf(f"x{c}{g}_raw", [P, PACK, WIDTH], F32)
+            rows = x[g * ROWS : (g + 1) * ROWS, c * WIDTH : (c + 1) * WIDTH]
+            nc.sync.dma_start(out=x_raw[c, g][:], in_=rows.rearrange("(p j) t -> p j t", j=PACK))
 
-        d_raw, d_grp, d_codes, d_scales = {}, {}, {}, {}
+        def interleave_x(c, g, engine):
+            x_grouped[c, g] = sbuf(f"x{c}{g}_grouped", [P, WIDTH, PACK], BF16)
+            interleave(engine, x_grouped[c, g][:], x_raw[c, g][:])
+
+        def quantise_x(c, g):
+            x_mx[c, g] = quantise(f"x{c}{g}", WIDTH, x_grouped[c, g][:].rearrange("p t j -> p (t j)"))
+
+        def x_tile(t, g):
+            codes, scales = x_mx[t // TILES_IN_CHUNK, g]
+            first = (t % TILES_IN_CHUNK) * P
+            return codes[:, first : first + P].bitcast(E4M3), scales[:, first : first + P]
+
+        down_raw, down_grouped, down_mx = {}, {}, {}
 
         def load_down(g):
-            raw = sb(f"dr{g}", [P, PACK, R], F32)
-            nc.sync.dma_start(out=raw[:], in_=down[g * 512 : (g + 1) * 512, :].rearrange("(p j) r -> p j r", j=PACK))
-            d_raw[g] = raw
+            down_raw[g] = sbuf(f"down{g}_raw", [P, PACK, R], F32)
+            rows = down[g * ROWS : (g + 1) * ROWS, :]
+            nc.sync.dma_start(out=down_raw[g][:], in_=rows.rearrange("(p j) r -> p j r", j=PACK))
 
-        u_raw, u_grp = {}, {}
-        u_codes = [sb(f"uc{i}", [P, HALF], U32) for i in range(2)]
-        u_scales = [sb(f"us{i}", [P, HALF], U8) for i in range(2)]
+        def interleave_down(g):
+            down_grouped[g] = sbuf(f"down{g}_grouped", [P, PACK, P, PACK], BF16)
+            grouped = down_grouped[g][:].rearrange("p i m j -> p m i j")
+            raw = down_raw[g][:].rearrange("p j (m i) -> p m i j", i=PACK)
+            middle = P // 2
+            copy(VECTOR, grouped[:, :middle], raw[:, :middle])
+            copy(SCALAR, grouped[:, middle:], raw[:, middle:])
+
+        def quantise_down(g):
+            down_mx[g] = quantise(f"down{g}", R, down_grouped[g][:].rearrange("p i m j -> p (i m j)"))
+
+        up_raw, up_grouped = {}, {}
+        up_codes = [sbuf(f"up{n}_codes", [P, HALF], U32) for n in range(2)]
+        up_scales = [sbuf(f"up{n}_scales", [P, HALF], U8) for n in range(2)]
 
         def load_up(q):
-            raw = sb(f"ur{q}", [P, PACK, UP_COLS], F32)
-            rows = up[:, q * UP_COLS : (q + 1) * UP_COLS]
-            nc.sync.dma_start(out=raw[:], in_=rows.rearrange("(p j) w -> p j w", j=PACK))
-            u_raw[q] = raw
+            up_raw[q] = sbuf(f"up{q}_raw", [P, PACK, WIDTH], F32)
+            rows = up[:, q * WIDTH : (q + 1) * WIDTH]
+            nc.sync.dma_start(out=up_raw[q][:], in_=rows.rearrange("(p j) n -> p j n", j=PACK))
+
+        def interleave_up(q, engine):
+            up_grouped[q] = sbuf(f"up{q}_grouped", [P, WIDTH, PACK], BF16)
+            interleave(engine, up_grouped[q][:], up_raw[q][:])
+
+        def quantise_up(q):
+            n, first = q // 2, (q % 2) * WIDTH
+            nc.vector.quantize_mx(
+                out=up_codes[n][:, first : first + WIDTH].bitcast(E4M3),
+                scales=up_scales[n][:, first : first + WIDTH],
+                in_=up_grouped[q][:].rearrange("p n j -> p (n j)"),
+            )
+
+        w4_codes = sbuf("w4_codes", [P, K_PASSES, 2 * N], U8)
+        w4_planes = sbuf("w4_planes", [P, K_PASSES, N], U8)
+
+        def load_w4():
+            for quadrant in range(4):
+                nc.sync.dma_start(
+                    out=w4_planes[32 * quadrant : 32 * quadrant + 4].bitcast(I32),
+                    in_=w4_scales[:, 4 * quadrant : 4 * quadrant + 4, :].rearrange("g s n -> s g n").bitcast(I32),
+                )
+            nc.sync.dma_start(out=w4_codes[:].bitcast(I32), in_=w4_words.rearrange("g p n -> p g n").bitcast(I32))
+
+        h_sums, h_grouped, h_mx = {}, {}, {}
+
+        def make_h(t):
+            h_sums[t] = take_bank(("h", t), f"h{t}_sums", [P, PACK, P])
+            for i in range(PACK):
+                for g in range(K_PASSES):
+                    down_codes, down_scales = down_mx[g]
+                    codes, scales = x_tile(t, g)
+                    nc.tensor.matmul_mx(
+                        out=h_sums[t][:, i, :],
+                        lhsT=down_codes[:, i * P : (i + 1) * P].bitcast(E4M3),
+                        lhsT_scale=down_scales[:, i * P : (i + 1) * P],
+                        rhs=codes,
+                        rhs_scale=scales,
+                        start=(g == 0),
+                        stop=(g == K_PASSES - 1),
+                    )
+
+        def empty_h(t, engine):
+            h_grouped[t] = sbuf(f"h{t}_grouped", [P, P, PACK], BF16)
+            copy(engine, h_grouped[t][:], h_sums[t][:].rearrange("p i t -> p t i"))
+            give_back(("h", t))
+
+        def quantise_h(t):
+            h_mx[t] = quantise(f"h{t}", P, h_grouped[t][:].rearrange("p t i -> p (t i)"))
+
+        sums = {}
+
+        def base(t, n):
+            sums[t, n] = take_bank((t, n), f"sums{t}{n}", [P, HALF])
+            for g in range(K_PASSES):
+                codes, scales = x_tile(t, g)
+                nc.tensor.matmul_mx(
+                    out=sums[t, n][:],
+                    lhsT=codes,
+                    lhsT_scale=scales,
+                    rhs=w4_codes[:, g, 2 * HALF * n : 2 * HALF * (n + 1)].bitcast(E2M1),
+                    rhs_scale=w4_planes[:, g, HALF * n : HALF * (n + 1)],
+                    start=(g == 0),
+                    stop=False,
+                )
+
+        def branch(t, n):
+            codes, scales = h_mx[t]
+            nc.tensor.matmul_mx(
+                out=sums[t, n][:],
+                lhsT=codes[:].bitcast(E4M3),
+                lhsT_scale=scales[:],
+                rhs=up_codes[n][:].bitcast(E4M3),
+                rhs_scale=up_scales[n][:],
+                start=False,
+                stop=True,
+            )
+
+        def finish(t, n, engine, parts=1):
+            width = HALF // parts
+            for i in range(parts):
+                part = sbuf(f"result{t}{n}{i}", [P, width], F32)
+                copy(engine, part[:], sums[t, n][:, i * width : (i + 1) * width])
+                first = n * HALF + i * width
+                nc.sync.dma_start(out=out[t * P : (t + 1) * P, first : first + width], in_=part[:])
+            give_back((t, n))
+
+        nc.vector.memset(w4_planes[:].rearrange("p g n -> p (g n)").bitcast(I32), 0)
 
         load_down(0)
         load_x(0, 0)
         load_x(0, 1)
         load_down(1)
-        for q in range(4):
-            nc.sync.dma_start(
-                out=w4s[32 * q : 32 * q + 4].bitcast(I32),
-                in_=w4_scales[:, 4 * q : 4 * q + 4, :].rearrange("g q n -> q g n").bitcast(I32),
-            )
-        nc.sync.dma_start(out=w4c[:].bitcast(I32), in_=w4_words.rearrange("g p n -> p g n").bitcast(I32))
+        load_w4()
         load_x(1, 0)
         load_x(1, 1)
         load_up(0)
@@ -84,235 +215,107 @@ def tile_mix_lowrank_tm_none_kernel(tc, x, w4_words, w4_scales, down, up, out):
         load_up(3)
         load_x(3, 1)
 
-        def copy(engine, out, in_):
-            if engine == S:
-                nc.scalar.copy(out=out, in_=in_)
-            else:
-                nc.vector.tensor_copy(out=out, in_=in_)
-
-        def interleave(engine, grp, raw):
-            copy(
-                engine,
-                grp[:].rearrange("p (c i) j -> p c j i", i=4),
-                raw[:].rearrange("p j (c i) -> p c j i", i=4),
-            )
-
-        def copy_x(c, g, engine):
-            grp = sb(f"xg{c}_{g}", [P, X_COLS, PACK], BF16)
-            interleave(engine, grp, x_raw[c, g])
-            x_grp[c, g] = grp
-
-        def quant_x(c, g):
-            codes = sb(f"xc{c}_{g}", [P, X_COLS], U32)
-            scales = sb(f"xs{c}_{g}", [P, X_COLS], U8)
-            nc.vector.quantize_mx(
-                out=codes[:].bitcast(E4M3), scales=scales[:], in_=x_grp[c, g][:].rearrange("p w j -> p (w j)")
-            )
-            x_codes[c, g], x_scales[c, g] = codes, scales
-
-        def copy_down(g):
-            grp = sb(f"dg{g}", [P, PACK, P, PACK], BF16)
-            src = d_raw[g][:].rearrange("p j (m i) -> p m i j", i=PACK)
-            dst = grp[:].rearrange("p i m j -> p m i j")
-            nc.vector.tensor_copy(out=dst[:, :DOWN_SPLIT], in_=src[:, :DOWN_SPLIT])
-            nc.scalar.copy(out=dst[:, DOWN_SPLIT:], in_=src[:, DOWN_SPLIT:])
-            d_grp[g] = grp
-
-        def quant_down(g):
-            codes = sb(f"dc{g}", [P, R], U32)
-            scales = sb(f"ds{g}", [P, R], U8)
-            nc.vector.quantize_mx(
-                out=codes[:].bitcast(E4M3), scales=scales[:], in_=d_grp[g][:].rearrange("p i m j -> p (i m j)")
-            )
-            d_codes[g], d_scales[g] = codes, scales
-
-        def copy_up(q, engine):
-            grp = sb(f"ug{q}", [P, UP_COLS, PACK], BF16)
-            interleave(engine, grp, u_raw[q])
-            u_grp[q] = grp
-
-        def quant_up(q):
-            cols = slice((q % 2) * UP_COLS, (q % 2 + 1) * UP_COLS)
-            nc.vector.quantize_mx(
-                out=u_codes[q // 2][:, cols].bitcast(E4M3),
-                scales=u_scales[q // 2][:, cols],
-                in_=u_grp[q][:].rearrange("p w j -> p (w j)"),
-            )
-
-        acc = {}
-        bank_of = {
-            (0, 0): 0, (1, 0): 4, (2, 0): 6, (3, 0): 2, (4, 0): 0, (5, 0): 4, (6, 0): 2, (7, 0): 1,
-            (0, 1): 1, (1, 1): 5, (2, 1): 3, (3, 1): 7, (4, 1): 6, (5, 1): 3, (6, 1): 7, (7, 1): 6,
-        }
-        h_bank = [2, 3, 3, 2, 0, 2, 2, 5]
-
-        def x_view(t, g):
-            c, first = divmod(t * P, X_COLS)
-            cols = slice(first, first + P)
-            return x_codes[c, g][:, cols].bitcast(E4M3), x_scales[c, g][:, cols]
-
-        def base(t, n):
-            acc[t, n] = acc_pool.tile([P, HALF], F32, name=f"acc{t}_{n}", tag=f"b{bank_of[t, n]}")
-            for g in range(K_PASSES):
-                codes, scales = x_view(t, g)
-                nc.tensor.matmul_mx(
-                    out=acc[t, n][:],
-                    lhsT=codes,
-                    lhsT_scale=scales,
-                    rhs=w4c[:, g, 2 * HALF * n : 2 * HALF * (n + 1)].bitcast(E2M1),
-                    rhs_scale=w4s[:, g, HALF * n : HALF * (n + 1)],
-                    start=(g == 0),
-                    stop=False,
-                )
-
-        h_codes, h_scales, h_ps, h_grp = {}, {}, {}, {}
-
-        def branch(t, n):
-            nc.tensor.matmul_mx(
-                out=acc[t, n][:],
-                lhsT=h_codes[t][:].bitcast(E4M3),
-                lhsT_scale=h_scales[t][:],
-                rhs=u_codes[n][:].bitcast(E4M3),
-                rhs_scale=u_scales[n][:],
-                start=False,
-                stop=True,
-            )
-
-        def make_h(t):
-            ps = acc_pool.tile([P, PACK, P], F32, name=f"hp{t}", tag=f"b{h_bank[t]}")
-            for i in range(PACK):
-                cols = slice(i * P, (i + 1) * P)
-                for g in range(K_PASSES):
-                    codes, scales = x_view(t, g)
-                    nc.tensor.matmul_mx(
-                        out=ps[:, i, :],
-                        lhsT=d_codes[g][:, cols].bitcast(E4M3),
-                        lhsT_scale=d_scales[g][:, cols],
-                        rhs=codes,
-                        rhs_scale=scales,
-                        start=(g == 0),
-                        stop=(g == K_PASSES - 1),
-                    )
-            h_ps[t] = ps
-
-        def copy_h(t, engine):
-            grp = sb(f"hg{t}", [P, P, PACK], BF16)
-            copy(engine, grp[:], h_ps[t][:].rearrange("p i t -> p t i"))
-            h_grp[t] = grp
-
-        def quant_h(t):
-            codes = sb(f"hc{t}", [P, P], U32)
-            scales = sb(f"hs{t}", [P, P], U8)
-            nc.vector.quantize_mx(
-                out=codes[:].bitcast(E4M3), scales=scales[:], in_=h_grp[t][:].rearrange("p t i -> p (t i)")
-            )
-            h_codes[t], h_scales[t] = codes, scales
-
-        def finish(t, n, engine, parts=1):
-            width = HALF // parts
-            for i in range(parts):
-                res = sb(f"o{t}_{n}_{i}", [P, width], F32)
-                copy(engine, res[:], acc[t, n][:, i * width : (i + 1) * width])
-                first = n * HALF + i * width
-                nc.sync.dma_start(out=out[t * P : (t + 1) * P, first : first + width], in_=res[:])
-
-        copy_down(0)
-        quant_down(0)
-        copy_x(0, 0, S)
-        copy_x(0, 1, V)
-        quant_x(0, 0)
-        quant_x(0, 1)
-        copy_down(1)
+        interleave_down(0)
+        quantise_down(0)
+        interleave_x(0, 0, SCALAR)
+        interleave_x(0, 1, VECTOR)
+        quantise_x(0, 0)
+        quantise_x(0, 1)
+        interleave_down(1)
         base(0, 0)
-        quant_down(1)
+        quantise_down(1)
         base(0, 1)
-        copy_x(1, 0, S)
+
+        interleave_x(1, 0, SCALAR)
         make_h(0)
-        copy_x(1, 1, V)
+        interleave_x(1, 1, VECTOR)
         make_h(1)
-        copy_h(0, S)
+        empty_h(0, SCALAR)
         base(1, 0)
-        quant_x(1, 0)
-        copy_h(1, S)
+        quantise_x(1, 0)
+        empty_h(1, SCALAR)
         base(1, 1)
-        quant_x(1, 1)
-        quant_h(0)
-        copy_up(0, S)
-        quant_h(1)
+        quantise_x(1, 1)
+        quantise_h(0)
+        interleave_up(0, SCALAR)
+        quantise_h(1)
         base(2, 0)
-        copy_up(1, V)
+        interleave_up(1, VECTOR)
         base(3, 1)
         make_h(3)
-        quant_up(0)
-        copy_x(2, 0, S)
-        quant_up(1)
+        quantise_up(0)
+
+        interleave_x(2, 0, SCALAR)
+        quantise_up(1)
         make_h(2)
-        copy_h(3, V)
+        empty_h(3, VECTOR)
         branch(0, 0)
         branch(1, 0)
-        copy_x(2, 1, V)
-        copy_h(2, S)
+        interleave_x(2, 1, VECTOR)
+        empty_h(2, SCALAR)
         base(3, 0)
-        quant_h(3)
-        finish(0, 0, S)
-        quant_h(2)
+        quantise_h(3)
+        finish(0, 0, SCALAR)
+        quantise_h(2)
         branch(3, 0)
-        quant_x(2, 0)
+        quantise_x(2, 0)
         branch(2, 0)
-        finish(1, 0, S)
-        quant_x(2, 1)
+        finish(1, 0, SCALAR)
+        quantise_x(2, 1)
         base(2, 1)
-        copy_up(2, V)
-        finish(2, 0, S)
+
+        interleave_up(2, VECTOR)
+        finish(2, 0, SCALAR)
         make_h(4)
-        finish(3, 0, S)
+        finish(3, 0, SCALAR)
         base(5, 0)
-        quant_up(2)
+        quantise_up(2)
         base(4, 1)
-        copy_up(3, V)
-        copy_h(4, S)
+        interleave_up(3, VECTOR)
+        empty_h(4, SCALAR)
         make_h(5)
-        copy_x(3, 0, S)
-        quant_up(3)
+        interleave_x(3, 0, SCALAR)
+        quantise_up(3)
         base(4, 0)
-        quant_h(4)
-        copy_x(3, 1, V)
+        quantise_h(4)
+        interleave_x(3, 1, VECTOR)
         branch(3, 1)
         branch(2, 1)
-        copy_h(5, S)
-        quant_x(3, 0)
+        empty_h(5, SCALAR)
+        quantise_x(3, 0)
         branch(0, 1)
         branch(1, 1)
-        quant_x(3, 1)
-        finish(3, 1, S)
+        quantise_x(3, 1)
+        finish(3, 1, SCALAR)
         branch(4, 1)
-        finish(1, 1, V)
+        finish(1, 1, VECTOR)
         branch(4, 0)
-        finish(0, 1, S)
+        finish(0, 1, SCALAR)
+
         make_h(6)
-        quant_h(5)
+        quantise_h(5)
         base(6, 1)
-        finish(4, 1, S)
-        copy_h(6, V)
+        finish(4, 1, SCALAR)
+        empty_h(6, VECTOR)
         make_h(7)
-        finish(2, 1, S)
-        quant_h(6)
+        finish(2, 1, SCALAR)
+        quantise_h(6)
         base(7, 0)
-        copy_h(7, S)
+        empty_h(7, SCALAR)
         branch(6, 1)
         base(7, 1)
-        finish(4, 0, S)
-        finish(6, 1, V)
+        finish(4, 0, SCALAR)
+        finish(6, 1, VECTOR)
         branch(5, 0)
-        quant_h(7)
+        quantise_h(7)
         base(5, 1)
-        finish(5, 0, S)
+        finish(5, 0, SCALAR)
         branch(7, 1)
         branch(7, 0)
-        finish(7, 1, V)
+        finish(7, 1, VECTOR)
         branch(5, 1)
-        finish(7, 0, S)
+        finish(7, 0, SCALAR)
         base(6, 0)
-        finish(5, 1, V)
+        finish(5, 1, VECTOR)
         branch(6, 0)
-        finish(6, 0, V, parts=2)
+        finish(6, 0, VECTOR, parts=2)

from contextlib import ExitStack

import concourse.mybir as mybir

K, R, N, T = 1024, 512, 1024, 1024
FLOPS = 2 * (K * R * T + K * N * T + R * N * T)

F32 = mybir.dt.float32
BF16 = mybir.dt.bfloat16
I32 = mybir.dt.int32
U32 = mybir.dt.uint32
U8 = mybir.dt.uint8
E4M3 = mybir.dt.float8_e4m3fn_x4
E2M1 = mybir.dt.float4_e2m1fn_x4

P = 128
PACK = 4
ROWS = P * PACK
K_PASSES = K // ROWS
WIDTH = 256
TILES_IN_CHUNK = WIDTH // P
HALF = 512
BANKS = 8


def tile_mix_lowrank_tm_none_kernel(tc, x, w4_words, w4_scales, down, up, out):
    nc = tc.nc
    SCALAR, VECTOR = "scalar", "vector"

    with ExitStack() as ctx:
        keep = ctx.enter_context(tc.tile_pool(name="keep", bufs=1))
        psum = ctx.enter_context(tc.psum_pool(name="psum", bufs=1))
        ctx.enter_context(tc.manual_schedule())

        def sbuf(name, shape, dtype):
            return keep.tile(shape, dtype, name=name, tag=name, align_bytes=64)

        free_banks = list(range(BANKS))
        bank_of = {}

        def take_bank(key, name, shape):
            bank_of[key] = free_banks[0]
            free_banks.remove(bank_of[key])
            return psum.tile(shape, F32, name=name, tag=f"bank{bank_of[key]}")

        def give_back(key):
            free_banks.append(bank_of[key])

        def copy(engine, dst, src):
            if engine == SCALAR:
                nc.scalar.copy(out=dst, in_=src)
            else:
                nc.vector.tensor_copy(out=dst, in_=src)

        def quantise(name, width, grouped):
            codes = sbuf(f"{name}_codes", [P, width], U32)
            scales = sbuf(f"{name}_scales", [P, width], U8)
            nc.vector.quantize_mx(out=codes[:].bitcast(E4M3), scales=scales[:], in_=grouped)
            return codes, scales

        def interleave(engine, grouped, raw):
            copy(
                engine,
                grouped.rearrange("p (c i) j -> p c j i", i=4),
                raw.rearrange("p j (c i) -> p c j i", i=4),
            )

        x_raw, x_grouped, x_mx = {}, {}, {}

        def load_x(c, g):
            x_raw[c, g] = sbuf(f"x{c}{g}_raw", [P, PACK, WIDTH], F32)
            rows = x[g * ROWS : (g + 1) * ROWS, c * WIDTH : (c + 1) * WIDTH]
            nc.sync.dma_start(out=x_raw[c, g][:], in_=rows.rearrange("(p j) t -> p j t", j=PACK))

        def interleave_x(c, g, engine):
            x_grouped[c, g] = sbuf(f"x{c}{g}_grouped", [P, WIDTH, PACK], BF16)
            interleave(engine, x_grouped[c, g][:], x_raw[c, g][:])

        def quantise_x(c, g):
            x_mx[c, g] = quantise(f"x{c}{g}", WIDTH, x_grouped[c, g][:].rearrange("p t j -> p (t j)"))

        def x_tile(t, g):
            codes, scales = x_mx[t // TILES_IN_CHUNK, g]
            first = (t % TILES_IN_CHUNK) * P
            return codes[:, first : first + P].bitcast(E4M3), scales[:, first : first + P]

        down_raw, down_grouped, down_mx = {}, {}, {}

        def load_down(g):
            down_raw[g] = sbuf(f"down{g}_raw", [P, PACK, R], F32)
            rows = down[g * ROWS : (g + 1) * ROWS, :]
            nc.sync.dma_start(out=down_raw[g][:], in_=rows.rearrange("(p j) r -> p j r", j=PACK))

        def interleave_down(g):
            down_grouped[g] = sbuf(f"down{g}_grouped", [P, PACK, P, PACK], BF16)
            grouped = down_grouped[g][:].rearrange("p i m j -> p m i j")
            raw = down_raw[g][:].rearrange("p j (m i) -> p m i j", i=PACK)
            middle = P // 2
            copy(VECTOR, grouped[:, :middle], raw[:, :middle])
            copy(SCALAR, grouped[:, middle:], raw[:, middle:])

        def quantise_down(g):
            down_mx[g] = quantise(f"down{g}", R, down_grouped[g][:].rearrange("p i m j -> p (i m j)"))

        up_raw, up_grouped = {}, {}
        up_codes = [sbuf(f"up{n}_codes", [P, HALF], U32) for n in range(2)]
        up_scales = [sbuf(f"up{n}_scales", [P, HALF], U8) for n in range(2)]

        def load_up(q):
            up_raw[q] = sbuf(f"up{q}_raw", [P, PACK, WIDTH], F32)
            rows = up[:, q * WIDTH : (q + 1) * WIDTH]
            nc.sync.dma_start(out=up_raw[q][:], in_=rows.rearrange("(p j) n -> p j n", j=PACK))

        def interleave_up(q, engine):
            up_grouped[q] = sbuf(f"up{q}_grouped", [P, WIDTH, PACK], BF16)
            interleave(engine, up_grouped[q][:], up_raw[q][:])

        def quantise_up(q):
            n, first = q // 2, (q % 2) * WIDTH
            nc.vector.quantize_mx(
                out=up_codes[n][:, first : first + WIDTH].bitcast(E4M3),
                scales=up_scales[n][:, first : first + WIDTH],
                in_=up_grouped[q][:].rearrange("p n j -> p (n j)"),
            )

        w4_codes = sbuf("w4_codes", [P, K_PASSES, 2 * N], U8)
        w4_planes = sbuf("w4_planes", [P, K_PASSES, N], U8)

        def load_w4():
            for quadrant in range(4):
                nc.sync.dma_start(
                    out=w4_planes[32 * quadrant : 32 * quadrant + 4].bitcast(I32),
                    in_=w4_scales[:, 4 * quadrant : 4 * quadrant + 4, :].rearrange("g s n -> s g n").bitcast(I32),
                )
            nc.sync.dma_start(out=w4_codes[:].bitcast(I32), in_=w4_words.rearrange("g p n -> p g n").bitcast(I32))

        h_sums, h_grouped, h_mx = {}, {}, {}

        def make_h(t):
            h_sums[t] = take_bank(("h", t), f"h{t}_sums", [P, PACK, P])
            for i in range(PACK):
                for g in range(K_PASSES):
                    down_codes, down_scales = down_mx[g]
                    codes, scales = x_tile(t, g)
                    nc.tensor.matmul_mx(
                        out=h_sums[t][:, i, :],
                        lhsT=down_codes[:, i * P : (i + 1) * P].bitcast(E4M3),
                        lhsT_scale=down_scales[:, i * P : (i + 1) * P],
                        rhs=codes,
                        rhs_scale=scales,
                        start=(g == 0),
                        stop=(g == K_PASSES - 1),
                    )

        def empty_h(t, engine):
            h_grouped[t] = sbuf(f"h{t}_grouped", [P, P, PACK], BF16)
            copy(engine, h_grouped[t][:], h_sums[t][:].rearrange("p i t -> p t i"))
            give_back(("h", t))

        def quantise_h(t):
            h_mx[t] = quantise(f"h{t}", P, h_grouped[t][:].rearrange("p t i -> p (t i)"))

        sums = {}

        def base(t, n):
            sums[t, n] = take_bank((t, n), f"sums{t}{n}", [P, HALF])
            for g in range(K_PASSES):
                codes, scales = x_tile(t, g)
                nc.tensor.matmul_mx(
                    out=sums[t, n][:],
                    lhsT=codes,
                    lhsT_scale=scales,
                    rhs=w4_codes[:, g, 2 * HALF * n : 2 * HALF * (n + 1)].bitcast(E2M1),
                    rhs_scale=w4_planes[:, g, HALF * n : HALF * (n + 1)],
                    start=(g == 0),
                    stop=False,
                )

        def branch(t, n):
            codes, scales = h_mx[t]
            nc.tensor.matmul_mx(
                out=sums[t, n][:],
                lhsT=codes[:].bitcast(E4M3),
                lhsT_scale=scales[:],
                rhs=up_codes[n][:].bitcast(E4M3),
                rhs_scale=up_scales[n][:],
                start=False,
                stop=True,
            )

        def finish(t, n, engine, parts=1):
            width = HALF // parts
            for i in range(parts):
                part = sbuf(f"result{t}{n}{i}", [P, width], F32)
                copy(engine, part[:], sums[t, n][:, i * width : (i + 1) * width])
                first = n * HALF + i * width
                nc.sync.dma_start(out=out[t * P : (t + 1) * P, first : first + width], in_=part[:])
            give_back((t, n))

        nc.vector.memset(w4_planes[:].rearrange("p g n -> p (g n)").bitcast(I32), 0)

        load_down(0)
        load_x(0, 0)
        load_x(0, 1)
        load_down(1)
        load_w4()
        load_x(1, 0)
        load_x(1, 1)
        load_up(0)
        load_up(1)
        load_x(2, 0)
        load_x(2, 1)
        load_x(3, 0)
        load_up(2)
        load_up(3)
        load_x(3, 1)

        interleave_down(0)
        quantise_down(0)
        interleave_x(0, 0, SCALAR)
        interleave_x(0, 1, VECTOR)
        quantise_x(0, 0)
        quantise_x(0, 1)
        interleave_down(1)
        base(0, 0)
        quantise_down(1)
        base(0, 1)

        interleave_x(1, 0, SCALAR)
        make_h(0)
        interleave_x(1, 1, VECTOR)
        make_h(1)
        empty_h(0, SCALAR)
        base(1, 0)
        quantise_x(1, 0)
        empty_h(1, SCALAR)
        base(1, 1)
        quantise_x(1, 1)
        quantise_h(0)
        interleave_up(0, SCALAR)
        quantise_h(1)
        base(2, 0)
        interleave_up(1, VECTOR)
        base(3, 1)
        make_h(3)
        quantise_up(0)

        interleave_x(2, 0, SCALAR)
        quantise_up(1)
        make_h(2)
        empty_h(3, VECTOR)
        branch(0, 0)
        branch(1, 0)
        interleave_x(2, 1, VECTOR)
        empty_h(2, SCALAR)
        base(3, 0)
        quantise_h(3)
        finish(0, 0, SCALAR)
        quantise_h(2)
        branch(3, 0)
        quantise_x(2, 0)
        branch(2, 0)
        finish(1, 0, SCALAR)
        quantise_x(2, 1)
        base(2, 1)

        interleave_up(2, VECTOR)
        finish(2, 0, SCALAR)
        make_h(4)
        finish(3, 0, SCALAR)
        base(5, 0)
        quantise_up(2)
        base(4, 1)
        interleave_up(3, VECTOR)
        empty_h(4, SCALAR)
        make_h(5)
        interleave_x(3, 0, SCALAR)
        quantise_up(3)
        base(4, 0)
        quantise_h(4)
        interleave_x(3, 1, VECTOR)
        branch(3, 1)
        branch(2, 1)
        empty_h(5, SCALAR)
        quantise_x(3, 0)
        branch(0, 1)
        branch(1, 1)
        quantise_x(3, 1)
        finish(3, 1, SCALAR)
        branch(4, 1)
        finish(1, 1, VECTOR)
        branch(4, 0)
        finish(0, 1, SCALAR)

        make_h(6)
        quantise_h(5)
        base(6, 1)
        finish(4, 1, SCALAR)
        empty_h(6, VECTOR)
        make_h(7)
        finish(2, 1, SCALAR)
        quantise_h(6)
        base(7, 0)
        empty_h(7, SCALAR)
        branch(6, 1)
        base(7, 1)
        finish(4, 0, SCALAR)
        finish(6, 1, VECTOR)
        branch(5, 0)
        quantise_h(7)
        base(5, 1)
        finish(5, 0, SCALAR)
        branch(7, 1)
        branch(7, 0)
        finish(7, 1, VECTOR)
        branch(5, 1)
        finish(7, 0, SCALAR)
        base(6, 0)
        finish(5, 1, VECTOR)
        branch(6, 0)
        finish(6, 0, VECTOR, parts=2)
